import numpy as np
import ml_dtypes


def mxq(x, axis, fmt="e4m3"):
    dtype, down = {"e4m3": (ml_dtypes.float8_e4m3fn, 7), "e5m2": (ml_dtypes.float8_e5m2, 14)}[fmt]
    v = np.moveaxis(np.asarray(x, np.float32).astype(ml_dtypes.bfloat16).astype(np.float64), axis, -1)
    blocks = v.reshape(v.shape[:-1] + (-1, 32))
    amax = np.abs(blocks).max(-1, keepdims=True)
    byte = np.maximum(np.where(amax > 0, np.frexp(amax)[1] - 1 + 127, 0) - down, 1)
    scale = np.exp2(byte - 127.0)
    codes = (blocks / scale).astype(np.float32).astype(dtype).astype(np.float64)
    return np.moveaxis((codes * scale).reshape(v.shape), -1, axis)


WIDE = False


def mx_kscale(k):
    if not WIDE:
        return np.ones(k)
    levels = np.array([30, -30])
    if k % 512:
        return np.exp2(np.random.permutation(np.resize(levels, k // 32))).repeat(32)
    a = np.empty((k // 512, 16))
    for p in range(k // 512):
        a[p, :8] = np.random.permutation(np.resize(levels, 8))
        for g in range(8):
            far = levels[np.abs(levels - a[p, g]) >= 10]
            a[p, g + 8] = far[np.random.randint(len(far))]
    return np.exp2(a.ravel()).repeat(32)


BF16 = ml_dtypes.bfloat16


def bf(x):
    return np.asarray(x, np.float32).astype(BF16)


def f64(x):
    return np.asarray(x).astype(np.float64)


E2M1 = np.array([0.0, 0.5, 1.0, 1.5, 2.0, 3.0, 4.0, 6.0, -0.0, -0.5, -1.0, -1.5, -2.0, -3.0, -4.0, -6.0])


def pack_weight(w, fmt):
    k, n = w.shape
    w = f64(bf(w)).reshape(k // 32, 32, n)
    amax = np.abs(w).max(1)
    if fmt in ("e4m3", "e5m2"):
        byte = np.frexp(amax)[1] - 1 + 127 - (7 if fmt == "e4m3" else 14)
    else:
        mant, ex = np.frexp(amax / 6.0)
        byte = np.where(mant > 0.5, ex, ex - 1) + 127
    byte = np.clip(np.where(amax > 0, byte, 1), 1, 254)
    scaled = (w * np.exp2(127.0 - byte)[:, None, :]).reshape(k, n).astype(np.float32)
    by_word = np.ascontiguousarray(scaled.reshape(k // 512, 128, 4, n).transpose(0, 1, 3, 2))
    if fmt in ("e4m3", "e5m2"):
        words = by_word.astype(ml_dtypes.float8_e4m3fn if fmt == "e4m3" else ml_dtypes.float8_e5m2).view(np.uint8)
    else:
        c = by_word.astype(ml_dtypes.float4_e2m1fn).view(np.uint8) & 0xF
        words = c[..., 0::2] | (c[..., 1::2] << 4)
    return np.ascontiguousarray(words), np.ascontiguousarray(byte.astype(np.uint8).reshape(k // 512, 16, n))


def unpack_weight(words, scales, fmt):
    g, p, n, _ = words.shape
    if fmt in ("e4m3", "e5m2"):
        vals = np.ascontiguousarray(words).view(ml_dtypes.float8_e4m3fn if fmt == "e4m3" else ml_dtypes.float8_e5m2).astype(np.float64)
    else:
        nib = np.empty((g, p, n, 4), np.uint8)
        nib[..., 0::2] = words & 0xF
        nib[..., 1::2] = words >> 4
        vals = E2M1[nib]
    vals = vals * np.repeat(np.exp2(scales.astype(np.float64) - 127.0), 8, axis=1)[..., None]
    return vals.transpose(0, 1, 3, 2).reshape(g * 512, n)

def planes(Y):
    n, m = Y.shape
    b = f64(bf(Y)).reshape(n // 32, 32, m)
    amax = np.abs(b).max(1)
    byte = np.clip(np.where(amax > 0, np.frexp(amax)[1] - 1 + 127 - 7, 1), 1, 254)
    codes = (b * np.exp2(127.0 - byte)[:, None, :]).reshape(n, m).astype(np.float32).astype(ml_dtypes.float8_e4m3fn).view(np.uint8)
    words = codes.reshape(n // 512, 128, 4, m).transpose(0, 1, 3, 2)
    return np.ascontiguousarray(words), np.ascontiguousarray(byte.astype(np.uint8).reshape(n // 512, 16, m))


D, C, A = 1024, 1280, 1536
SPREAD = 0.8
WIDTH = 0.5


def setup_inputs():
    s = mx_kscale(D)
    g = np.random.randn(D, C) * np.exp(SPREAD * np.random.randn(D, C) - SPREAD ** 2)
    g_words, g_scales = pack_weight(g * s[:, None], "e5m2")
    target = WIDTH * np.random.randn(A, D) / np.sqrt(D)
    selected = WIDTH * np.random.randn(A, D) / np.sqrt(D)
    mass = np.exp(SPREAD * np.random.randn(A))
    return {"g_words": g_words, "g_scales": g_scales,
            "target": bf(target / s[None, :]),
            "selected": bf(selected / s[None, :]),
            "mass": bf(mass)}


def reference(g_words, g_scales, target, selected, mass):
    G = unpack_weight(g_words, g_scales, "e5m2")
    Tq = mxq(f64(target), 1, "e4m3")
    Sq = mxq(f64(selected), 1, "e4m3")
    P = G.T @ Tq.T
    Q = G.T @ Sq.T
    y = (np.exp(P) - np.exp(Q)) * f64(mass)
    Y = y.T
    words, scales = planes(Y)
    return y, words, scales

@@ -1,0 +1,250 @@
+from contextlib import ExitStack
+
+import concourse.mybir as mybir
+from concourse.masks import make_identity
+
+D, C, A = 1024, 1280, 1536
+FLOPS = 2 * 2 * D * C * A
+
+F32 = mybir.dt.float32
+BF16 = mybir.dt.bfloat16
+I32 = mybir.dt.int32
+U32 = mybir.dt.uint32
+U8 = mybir.dt.uint8
+E4M3X4 = mybir.dt.float8_e4m3fn_x4
+E5M2X4 = mybir.dt.float8_e5m2_x4
+EXP = mybir.ActivationFunctionType.Exp
+SUB = mybir.AluOpType.subtract
+MUL = mybir.AluOpType.mult
+
+P = 128
+PASSES = D // 512
+GROUP = 512
+GROUPS = A // GROUP
+HALF = GROUP // 2
+G_CHUNKS = [(0, 256), (256, 768), (768, 1280)]
+WORD_STORES = [(0, 512), (512, 1024), (1024, 1280)]
+
+
+def tile_mmd_witness_terms_k2_kernel(tc, g_words, g_scales, target, selected, mass, out_0, out_1, out_2):
+    nc = tc.nc
+    atoms = [target, selected]
+
+    steps = []
+    for g in range(GROUPS):
+        widths = [2, 2, 2, 2, 2] if g < GROUPS - 1 else [2, 2, 2, 2, 1, 1]
+        c0 = 0
+        for w in widths:
+            steps.append((g, c0, w))
+            c0 = c0 + w * P
+
+    with ExitStack() as ctx:
+        keep = ctx.enter_context(tc.tile_pool(name="keep", bufs=1))
+        work = ctx.enter_context(tc.tile_pool(name="work", bufs=2))
+        psum = ctx.enter_context(tc.psum_pool(name="psum", bufs=1))
+        ctx.enter_context(tc.manual_schedule())
+
+        ident = keep.tile([P, P], F32, name="ident")
+        make_identity(nc, ident[:])
+        warm_in = keep.tile([P, 1], F32, name="warm_in")
+        warm_out = keep.tile([P, 1], F32, name="warm_out")
+        nc.vector.memset(warm_in[:], 0.0)
+        nc.scalar.activation(out=warm_out[:], in_=warm_in[:], func=EXP)
+        g_sc = keep.tile([P, PASSES, C], U8, name="g_sc", align_bytes=64)
+        nc.vector.memset(g_sc[:].bitcast(I32), 0)
+
+        raw = {}
+        g_w = {}
+        mass_b = {}
+
+        def load_atoms(m, g, b):
+            t = keep.tile([P, 2, D], BF16, name="raw_%d_%d_%d" % (m, g, b), align_bytes=64)
+            a0 = g * GROUP + b * HALF
+            nc.sync.dma_start(out=t[:], in_=atoms[m][a0 : a0 + HALF, :].rearrange("(j r) k -> r j k", j=2))
+            raw[(m, g, b)] = t
+
+        def load_g_words(i):
+            lo, hi = G_CHUNKS[i]
+            t = keep.tile([P, PASSES, hi - lo], U32, name="g_w_%d" % i, align_bytes=64)
+            src = g_words.rearrange("h p n t -> p h (n t)")[:, :, 4 * lo : 4 * hi].bitcast(I32)
+            nc.sync.dma_start(out=t[:].bitcast(I32), in_=src)
+            g_w[i] = t
+
+        def load_g_scales():
+            for q in range(4):
+                src = g_scales[:, 4 * q : 4 * q + 4, :].rearrange("h r n -> r h n").bitcast(I32)
+                nc.sync.dma_start(out=g_sc[32 * q : 32 * q + 4, :, :].bitcast(I32), in_=src)
+
+        def load_mass(g):
+            t = keep.tile([P, GROUP], BF16, name="mass_%d" % g, align_bytes=64)
+            nc.sync.dma_start(out=t[:], in_=mass[g * GROUP : (g + 1) * GROUP].partition_broadcast(P))
+            mass_b[g] = t
+
+        for m in range(2):
+            for b in range(2):
+                load_atoms(m, 0, b)
+        load_g_words(0)
+        load_g_scales()
+        load_mass(0)
+        load_atoms(0, 1, 0)
+        load_g_words(1)
+        load_atoms(0, 1, 1)
+        load_atoms(1, 1, 0)
+        load_g_words(2)
+        load_atoms(1, 1, 1)
+        load_mass(1)
+        for m in range(2):
+            for b in range(2):
+                load_atoms(m, 2, b)
+        load_mass(2)
+
+        codes = {}
+        scales = {}
+        for m in range(2):
+            for g in range(GROUPS):
+                for h in range(PASSES):
+                    codes[(m, g, h)] = keep.tile([P, GROUP], U32, name="codes_%d_%d_%d" % (m, g, h), align_bytes=64)
+                    scales[(m, g, h)] = keep.tile([P, GROUP], U8, name="scales_%d_%d_%d" % (m, g, h), align_bytes=64)
+        y_words = [keep.tile([P, C], U32, name="y_words_%d" % g, align_bytes=64) for g in range(GROUPS)]
+        y_scales = [keep.tile([P, C], U8, name="y_scales_%d" % g, align_bytes=64) for g in range(GROUPS)]
+
+        banks = {}
+        staged = {}
+
+        def turn_atoms(key):
+            m, g, b, h = key
+            words = raw[(m, g, b)][:].bitcast(F32)
+            bank = psum.tile([P, 2, 2, P], F32, name="turned", bufs=3)
+            for j in range(2):
+                for u in range(2):
+                    nc.tensor.transpose(bank[:, j, u, :], words[:, j, 256 * h + u : 256 * (h + 1) : 2], ident[:])
+            banks[key] = bank
+
+        def copy_bank(key, w, on_vector):
+            t = work.tile([P, w * GROUP], BF16, name="staged", bufs=4, align_bytes=64)
+            dst = t[:].bitcast(F32).rearrange("p (j r u) -> p j r u", j=w, u=2)
+            src = banks[key][:].rearrange("p j u r -> p j r u")
+            if on_vector:
+                nc.vector.tensor_copy(out=dst, in_=src)
+            else:
+                nc.scalar.copy(out=dst, in_=src)
+            staged[key] = t
+
+        def quantise_atoms(key):
+            m, g, b, h = key
+            cols = slice(b * HALF, (b + 1) * HALF)
+            nc.vector.quantize_mx(out=codes[(m, g, h)][:, cols].bitcast(E4M3X4), scales=scales[(m, g, h)][:, cols], in_=staged[key][:])
+
+        exps = {}
+        diffs = {}
+        ys = {}
+        rounded = {}
+
+        def product_and_exp(i, m, j):
+            g, c0, w = steps[i]
+            if j == 0:
+                exps[(i, m)] = work.tile([P, w, GROUP], F32, name="exp_%d" % m, bufs=3)
+            c = c0 + j * P
+            chunk = [n for n, (lo, hi) in enumerate(G_CHUNKS) if lo <= c < hi][0]
+            off = c - G_CHUNKS[chunk][0]
+            acc = psum.tile([P, GROUP], F32, name="acc", bufs=5)
+            for h in range(PASSES):
+                nc.tensor.matmul_mx(
+                    out=acc[:],
+                    lhsT=g_w[chunk][:, h, off : off + P].bitcast(E5M2X4),
+                    lhsT_scale=g_sc[:, h, c : c + P],
+                    rhs=codes[(m, g, h)][:].bitcast(E4M3X4),
+                    rhs_scale=scales[(m, g, h)][:],
+                    start=(h == 0),
+                    stop=(h == PASSES - 1),
+                )
+            nc.scalar.activation(out=exps[(i, m)][:, j, :], in_=acc[:], func=EXP)
+
+        def subtract(i):
+            g, c0, w = steps[i]
+            d = work.tile([P, w, GROUP], F32, name="diff", bufs=2)
+            nc.vector.tensor_tensor(out=d[:], in0=exps[(i, 0)][:], in1=exps[(i, 1)][:], op=SUB)
+            diffs[i] = d
+
+        def weigh(i):
+            g, c0, w = steps[i]
+            y = work.tile([P, w, GROUP], F32, name="y", bufs=4)
+            nc.vector.tensor_tensor(out=y[:], in0=diffs[i][:], in1=mass_b[g][:].unsqueeze(1).to_broadcast([P, w, GROUP]), op=MUL)
+            nc.sync.dma_start(
+                out=out_0[c0 : c0 + w * P, g * GROUP : (g + 1) * GROUP].rearrange("(j c) a -> c j a", j=w), in_=y[:]
+            )
+            ys[i] = y
+
+        def round_y(i):
+            g, c0, w = steps[i]
+            t = work.tile([P, w, 2, P, 2], BF16, name="rounded", bufs=2, align_bytes=64)
+            nc.vector.tensor_copy(out=t[:], in_=ys[i][:].rearrange("c j (p u e) -> c j u p e", u=2, e=2))
+            rounded[i] = t
+
+        def turn_y(i):
+            g, c0, w = steps[i]
+            words = rounded[i][:].rearrange("c j u p e -> c j u (p e)").bitcast(F32)
+            bank = psum.tile([P, w, 2, P], F32, name="turned", bufs=3)
+            for j in range(w):
+                for u in range(2):
+                    nc.tensor.transpose(bank[:, j, u, :], words[:, j, u, :], ident[:])
+            banks[i] = bank
+
+        def quantise_y(i):
+            g, c0, w = steps[i]
+            cols = slice(c0, c0 + w * P)
+            nc.vector.quantize_mx(out=y_words[g][:, cols].bitcast(E4M3X4), scales=y_scales[g][:, cols], in_=staged[i][:])
+            for lo, hi in WORD_STORES:
+                if hi == c0 + w * P:
+                    dst = out_1[g].rearrange("p n t -> p (n t)")[:, 4 * lo : 4 * hi].bitcast(I32)
+                    nc.sync.dma_start(out=dst, in_=y_words[g][:, lo:hi].bitcast(I32))
+            if c0 + w * P == C:
+                for q in range(4):
+                    queue = nc.scalar if (g == GROUPS - 1 and q % 2 == 0) else nc.sync
+                    queue.dma_start(
+                        out=out_2[g, 4 * q : 4 * q + 4, :].bitcast(I32), in_=y_scales[g][32 * q : 32 * q + 4, :].bitcast(I32)
+                    )
+
+        def prep_keys(g):
+            return [(m, g, b, h) for m in range(2) for b in range(2) for h in range(PASSES)]
+
+        head = prep_keys(0)
+        for n in range(0, len(head), 2):
+            turn_atoms(head[n])
+            copy_bank(head[n], 2, False)
+            turn_atoms(head[n + 1])
+            copy_bank(head[n + 1], 2, True)
+            quantise_atoms(head[n])
+            quantise_atoms(head[n + 1])
+
+        turned_in = {}
+        for i, (g, c0, w) in enumerate(steps):
+            n = c0 // HALF
+            turned_in[i] = prep_keys(g + 1)[2 * n : 2 * n + 2] if g + 1 < GROUPS else []
+
+        last = len(steps) - 1
+        for i in range(len(steps) + 3):
+            copies = []
+            if 0 <= i - 3:
+                copies.append((i - 3, steps[i - 3][2]))
+            copies.extend([(key, 2) for key in turned_in.get(i - 1, [])])
+            products = [(m, j) for m in range(2) for j in range(steps[i][2])] if i <= last else []
+            for n in range(max(len(copies), len(products))):
+                if n < len(copies):
+                    copy_bank(copies[n][0], copies[n][1], False)
+                if n < len(products):
+                    product_and_exp(i, products[n][0], products[n][1])
+            if 0 <= i - 1 <= last:
+                subtract(i - 1)
+            if 0 <= i - 2 <= last:
+                round_y(i - 2)
+            if 0 <= i - 1 <= last:
+                weigh(i - 1)
+            if 0 <= i - 3:
+                quantise_y(i - 3)
+            for key in turned_in.get(i - 1, []):
+                quantise_atoms(key)
+            if 0 <= i - 2 <= last:
+                turn_y(i - 2)
+            for key in turned_in.get(i, []):
+                turn_atoms(key)

@@ -61,7 +61,16 @@ def tile_mmd_witness_terms_k2_kernel(tc, g_words, g_scales, target, selected, ma
             t = keep.tile([P, 2, D], BF16, name="raw_%d_%d_%d" % (m, g, b), align_bytes=64)
             a0 = g * GROUP + b * HALF
             nc.sync.dma_start(out=t[:], in_=atoms[m][a0 : a0 + HALF, :].rearrange("(j r) k -> r j k", j=2))
-            raw[(m, g, b)] = t
+            for h in range(PASSES):
+                raw[(m, g, b, h)] = t[:].bitcast(F32)[:, :, 256 * h : 256 * (h + 1)]
+
+        def load_pass(key):
+            m, g, b, h = key
+            t = keep.tile([P, 2, 512], BF16, name="raw_%d_%d_%d_%d" % key, align_bytes=64)
+            a0 = g * GROUP + b * HALF
+            src = atoms[m][a0 : a0 + HALF, 512 * h : 512 * (h + 1)]
+            nc.sync.dma_start(out=t[:], in_=src.rearrange("(j r) k -> r j k", j=2))
+            raw[key] = t[:].bitcast(F32)
 
         def load_g_words(i):
             lo, hi = G_CHUNKS[i]
@@ -80,15 +89,15 @@ def tile_mmd_witness_terms_k2_kernel(tc, g_words, g_scales, target, selected, ma
             nc.sync.dma_start(out=t[:], in_=mass[g * GROUP : (g + 1) * GROUP].partition_broadcast(P))
             mass_b[g] = t
 
-        for m in range(2):
-            for b in range(2):
-                load_atoms(m, 0, b)
+        head = [(m, 0, b, h) for m in range(2) for b in range(2) for h in range(PASSES)]
+        for key in head:
+            load_pass(key)
         load_g_words(0)
         load_g_scales()
         load_mass(0)
         load_atoms(0, 1, 0)
-        load_g_words(1)
         load_atoms(0, 1, 1)
+        load_g_words(1)
         load_atoms(1, 1, 0)
         load_g_words(2)
         load_atoms(1, 1, 1)
@@ -110,15 +119,20 @@ def tile_mmd_witness_terms_k2_kernel(tc, g_words, g_scales, target, selected, ma
 
         banks = {}
         staged = {}
+        ordered = {}
 
         def turn_atoms(key):
-            m, g, b, h = key
-            words = raw[(m, g, b)][:].bitcast(F32)
             bank = psum.tile([P, 2, 2, P], F32, name="turned", bufs=3)
             for j in range(2):
                 for u in range(2):
-                    nc.tensor.transpose(bank[:, j, u, :], words[:, j, 256 * h + u : 256 * (h + 1) : 2], ident[:])
+                    src = ordered[key][:, j, u, :] if key in ordered else raw[key][:, j, u : 256 : 2]
+                    nc.tensor.transpose(bank[:, j, u, :], src, ident[:])
             banks[key] = bank
+
+        def order_words(key):
+            t = work.tile([P, 2, 2, P], F32, name="ordered", bufs=3)
+            nc.vector.tensor_copy(out=t[:], in_=raw[key].rearrange("r j (p u) -> r j u p", u=2))
+            ordered[key] = t
 
         def copy_bank(key, w, on_vector):
             t = work.tile([P, w * GROUP], BF16, name="staged", bufs=4, align_bytes=64)
@@ -177,8 +191,12 @@ def tile_mmd_witness_terms_k2_kernel(tc, g_words, g_scales, target, selected, ma
 
         def round_y(i):
             g, c0, w = steps[i]
-            t = work.tile([P, w, 2, P, 2], BF16, name="rounded", bufs=2, align_bytes=64)
-            nc.vector.tensor_copy(out=t[:], in_=ys[i][:].rearrange("c j (p u e) -> c j u p e", u=2, e=2))
+            t = work.tile([P, w, 2, P, 2], BF16, name="rounded", bufs=3, align_bytes=64)
+            src = ys[i][:].rearrange("c j (p u e) -> c j u p e", u=2, e=2)
+            if i in [12,13,14]:
+                nc.scalar.copy(out=t[:], in_=src)
+            else:
+                nc.vector.tensor_copy(out=t[:], in_=src)
             rounded[i] = t
 
         def turn_y(i):
@@ -208,43 +226,50 @@ def tile_mmd_witness_terms_k2_kernel(tc, g_words, g_scales, target, selected, ma
         def prep_keys(g):
             return [(m, g, b, h) for m in range(2) for b in range(2) for h in range(PASSES)]
 
-        head = prep_keys(0)
-        for n in range(0, len(head), 2):
-            turn_atoms(head[n])
-            copy_bank(head[n], 2, False)
-            turn_atoms(head[n + 1])
-            copy_bank(head[n + 1], 2, True)
-            quantise_atoms(head[n])
-            quantise_atoms(head[n + 1])
+        order_words(head[0])
+        for n in range(len(head) + 1):
+            if n + 1 < len(head):
+                order_words(head[n + 1])
+            if n >= 1:
+                copy_bank(head[n - 1], 2, False)
+            if n >= 2:
+                quantise_atoms(head[n - 2])
+            if n < len(head):
+                turn_atoms(head[n])
+        quantise_atoms(head[-1])
 
+        pending = prep_keys(1) + prep_keys(2)
         turned_in = {}
-        for i, (g, c0, w) in enumerate(steps):
-            n = c0 // HALF
-            turned_in[i] = prep_keys(g + 1)[2 * n : 2 * n + 2] if g + 1 < GROUPS else []
+        to_order = pending[:6]
+        for i, n in enumerate([2,2,2,2,0,2,2,2,2]):
+            turned_in[i] = pending[:n]
+            pending = pending[n:]
 
         last = len(steps) - 1
-        for i in range(len(steps) + 3):
-            copies = []
-            if 0 <= i - 3:
-                copies.append((i - 3, steps[i - 3][2]))
-            copies.extend([(key, 2) for key in turned_in.get(i - 1, [])])
+        for i in range(len(steps) + 4):
+            copies = [(key, 2) for key in turned_in.get(i - 1, [])]
+            if 0 <= i - 4:
+                copies = copies + [(i - 4, steps[i - 4][2])]
             products = [(m, j) for m in range(2) for j in range(steps[i][2])] if i <= last else []
             for n in range(max(len(copies), len(products))):
                 if n < len(copies):
                     copy_bank(copies[n][0], copies[n][1], False)
                 if n < len(products):
                     product_and_exp(i, products[n][0], products[n][1])
+            for key in turned_in.get(i, []):
+                if key in to_order:
+                    order_words(key)
             if 0 <= i - 1 <= last:
                 subtract(i - 1)
             if 0 <= i - 2 <= last:
                 round_y(i - 2)
             if 0 <= i - 1 <= last:
                 weigh(i - 1)
-            if 0 <= i - 3:
-                quantise_y(i - 3)
             for key in turned_in.get(i - 1, []):
                 quantise_atoms(key)
-            if 0 <= i - 2 <= last:
-                turn_y(i - 2)
+            if 0 <= i - 4:
+                quantise_y(i - 4)
             for key in turned_in.get(i, []):
                 turn_atoms(key)
+            if 0 <= i - 3 <= last:
+                turn_y(i - 3)

@@ -23,7 +23,6 @@ GROUP = 512
 GROUPS = A // GROUP
 HALF = GROUP // 2
 G_CHUNKS = [(0, 256), (256, 768), (768, 1280)]
-WORD_STORES = [(0, 512), (512, 1024), (1024, 1280)]
 
 
 def tile_mmd_witness_terms_k2_kernel(tc, g_words, g_scales, target, selected, mass, out_0, out_1, out_2):
@@ -55,7 +54,6 @@ def tile_mmd_witness_terms_k2_kernel(tc, g_words, g_scales, target, selected, ma
 
         raw = {}
         g_w = {}
-        mass_b = {}
 
         def load_atoms(m, g, b):
             t = keep.tile([P, 2, D], BF16, name="raw_%d_%d_%d" % (m, g, b), align_bytes=64)
@@ -84,28 +82,23 @@ def tile_mmd_witness_terms_k2_kernel(tc, g_words, g_scales, target, selected, ma
                 src = g_scales[:, 4 * q : 4 * q + 4, :].rearrange("h r n -> r h n").bitcast(I32)
                 nc.sync.dma_start(out=g_sc[32 * q : 32 * q + 4, :, :].bitcast(I32), in_=src)
 
-        def load_mass(g):
-            t = keep.tile([P, GROUP], BF16, name="mass_%d" % g, align_bytes=64)
-            nc.sync.dma_start(out=t[:], in_=mass[g * GROUP : (g + 1) * GROUP].partition_broadcast(P))
-            mass_b[g] = t
+        mass_cols = keep.tile([P, GROUPS, 4], BF16, name="mass_cols", align_bytes=64)
+        nc.sync.dma_start(out=mass_cols[:], in_=mass.rearrange("(g r e) -> r g e", g=GROUPS, e=4))
 
         head = [(m, 0, b, h) for m in range(2) for b in range(2) for h in range(PASSES)]
         for key in head:
             load_pass(key)
         load_g_words(0)
         load_g_scales()
-        load_mass(0)
         load_atoms(0, 1, 0)
         load_atoms(0, 1, 1)
         load_g_words(1)
         load_atoms(1, 1, 0)
         load_g_words(2)
         load_atoms(1, 1, 1)
-        load_mass(1)
         for m in range(2):
             for b in range(2):
                 load_atoms(m, 2, b)
-        load_mass(2)
 
         codes = {}
         scales = {}
@@ -134,30 +127,51 @@ def tile_mmd_witness_terms_k2_kernel(tc, g_words, g_scales, target, selected, ma
             nc.vector.tensor_copy(out=t[:], in_=raw[key].rearrange("r j (p u) -> r j u p", u=2))
             ordered[key] = t
 
-        def copy_bank(key, w, on_vector):
-            t = work.tile([P, w * GROUP], BF16, name="staged", bufs=4, align_bytes=64)
-            dst = t[:].bitcast(F32).rearrange("p (j r u) -> p j r u", j=w, u=2)
-            src = banks[key][:].rearrange("p j u r -> p j r u")
+        def copy_bank(bank, dst, on_vector):
+            w = bank.shape[1]
+            dst = dst.bitcast(F32).rearrange("p (j r u) -> p j r u", j=w, u=2)
+            src = bank.rearrange("p j u r -> p j r u")
             if on_vector:
                 nc.vector.tensor_copy(out=dst, in_=src)
             else:
                 nc.scalar.copy(out=dst, in_=src)
-            staged[key] = t
 
-        def quantise_atoms(key):
+        def copy_atoms(key, on_vector):
             m, g, b, h = key
-            cols = slice(b * HALF, (b + 1) * HALF)
-            nc.vector.quantize_mx(out=codes[(m, g, h)][:, cols].bitcast(E4M3X4), scales=scales[(m, g, h)][:, cols], in_=staged[key][:])
+            if (m, g, h) not in staged:
+                staged[(m, g, h)] = work.tile([P, 2, 4 * HALF], BF16, name="staged", bufs=3, align_bytes=64)
+            copy_bank(banks[key][:], staged[(m, g, h)][:, b, :], on_vector)
+
+        def quantise_atoms(m, g, h, b0, b1):
+            cols = slice(b0 * HALF, b1 * HALF)
+            src = staged[(m, g, h)][:, b0:b1, :].rearrange("p b n -> p (b n)")
+            nc.vector.quantize_mx(out=codes[(m, g, h)][:, cols].bitcast(E4M3X4), scales=scales[(m, g, h)][:, cols], in_=src)
+
+        mass_b = keep.tile([P, A], BF16, name="mass_b", align_bytes=64)
+        for g0, g1 in ((0, 2), (2, 3)):
+            bank = psum.tile([P, g1 - g0, 2, P], F32, name="turned", bufs=3)
+            for g in range(g0, g1):
+                for u in range(2):
+                    nc.tensor.transpose(bank[:, g - g0, u, :], mass_cols[:].bitcast(F32)[:, g, u : u + 1].to_broadcast([P, P]), ident[:])
+            copy_bank(bank[:], mass_b[:, g0 * GROUP : g1 * GROUP], False)
 
         exps = {}
-        diffs = {}
         ys = {}
+        diffs = {}
         rounded = {}
+        y_staged = {}
+        blocks = [[n] for n in range(16)]
+        block_of = {i: k for k, blk in enumerate(blocks) for i in blk}
+
+        def span(k):
+            g, c0, w = steps[blocks[k][0]]
+            return g, c0, sum(steps[i][2] for i in blocks[k])
 
         def product_and_exp(i, m, j):
             g, c0, w = steps[i]
-            if j == 0:
-                exps[(i, m)] = work.tile([P, w, GROUP], F32, name="exp_%d" % m, bufs=3)
+            k = block_of[i]
+            if (k, m) not in exps:
+                exps[(k, m)] = work.tile([P, span(k)[2], GROUP], F32, name="exp_%d" % m, bufs=3)
             c = c0 + j * P
             chunk = [n for n, (lo, hi) in enumerate(G_CHUNKS) if lo <= c < hi][0]
             off = c - G_CHUNKS[chunk][0]
@@ -172,104 +186,131 @@ def tile_mmd_witness_terms_k2_kernel(tc, g_words, g_scales, target, selected, ma
                     start=(h == 0),
                     stop=(h == PASSES - 1),
                 )
-            nc.scalar.activation(out=exps[(i, m)][:, j, :], in_=acc[:], func=EXP)
+            nc.scalar.activation(out=exps[(k, m)][:, (c - span(k)[1]) // P, :], in_=acc[:], func=EXP)
 
-        def subtract(i):
-            g, c0, w = steps[i]
-            d = work.tile([P, w, GROUP], F32, name="diff", bufs=2)
-            nc.vector.tensor_tensor(out=d[:], in0=exps[(i, 0)][:], in1=exps[(i, 1)][:], op=SUB)
-            diffs[i] = d
+        def subtract(k):
+            g, c0, w = span(k)
+            diffs[k] = work.tile([P, w, GROUP], F32, name="diff", bufs=1)
+            nc.vector.tensor_tensor(out=diffs[k][:], in0=exps[(k, 0)][:], in1=exps[(k, 1)][:], op=SUB)
 
-        def weigh(i):
-            g, c0, w = steps[i]
-            y = work.tile([P, w, GROUP], F32, name="y", bufs=4)
-            nc.vector.tensor_tensor(out=y[:], in0=diffs[i][:], in1=mass_b[g][:].unsqueeze(1).to_broadcast([P, w, GROUP]), op=MUL)
+        def weigh(k):
+            g, c0, w = span(k)
+            ys[k] = work.tile([P, w, GROUP], F32, name="y", bufs=3)
+            row = mass_b[:, g * GROUP : (g + 1) * GROUP]
+            nc.vector.tensor_tensor(out=ys[k][:], in0=diffs[k][:], in1=row.unsqueeze(1).to_broadcast([P, w, GROUP]), op=MUL)
             nc.sync.dma_start(
-                out=out_0[c0 : c0 + w * P, g * GROUP : (g + 1) * GROUP].rearrange("(j c) a -> c j a", j=w), in_=y[:]
+                out=out_0[c0 : c0 + w * P, g * GROUP : (g + 1) * GROUP].rearrange("(j c) a -> c j a", j=w), in_=ys[k][:]
             )
-            ys[i] = y
 
-        def round_y(i):
-            g, c0, w = steps[i]
-            t = work.tile([P, w, 2, P, 2], BF16, name="rounded", bufs=3, align_bytes=64)
-            src = ys[i][:].rearrange("c j (p u e) -> c j u p e", u=2, e=2)
-            if i in [12,13,14]:
-                nc.scalar.copy(out=t[:], in_=src)
+        def round_y(k):
+            g, c0, w = span(k)
+            rounded[k] = work.tile([P, w, 2, P, 2], BF16, name="rounded", bufs=2, align_bytes=64)
+            src = ys[k][:].rearrange("c j (p u e) -> c j u p e", u=2, e=2)
+            if k in [12,13,14]:
+                nc.scalar.copy(out=rounded[k][:], in_=src)
             else:
-                nc.vector.tensor_copy(out=t[:], in_=src)
-            rounded[i] = t
+                nc.vector.tensor_copy(out=rounded[k][:], in_=src)
 
         def turn_y(i):
             g, c0, w = steps[i]
-            words = rounded[i][:].rearrange("c j u p e -> c j u (p e)").bitcast(F32)
+            k = block_of[i]
+            j0 = (c0 - span(k)[1]) // P
+            words = rounded[k][:].rearrange("c j u p e -> c j u (p e)").bitcast(F32)
             bank = psum.tile([P, w, 2, P], F32, name="turned", bufs=3)
             for j in range(w):
                 for u in range(2):
-                    nc.tensor.transpose(bank[:, j, u, :], words[:, j, u, :], ident[:])
+                    nc.tensor.transpose(bank[:, j, u, :], words[:, j0 + j, u, :], ident[:])
             banks[i] = bank
 
-        def quantise_y(i):
+        def copy_y(i, on_vector):
             g, c0, w = steps[i]
-            cols = slice(c0, c0 + w * P)
-            nc.vector.quantize_mx(out=y_words[g][:, cols].bitcast(E4M3X4), scales=y_scales[g][:, cols], in_=staged[i][:])
-            for lo, hi in WORD_STORES:
-                if hi == c0 + w * P:
-                    dst = out_1[g].rearrange("p n t -> p (n t)")[:, 4 * lo : 4 * hi].bitcast(I32)
-                    nc.sync.dma_start(out=dst, in_=y_words[g][:, lo:hi].bitcast(I32))
-            if c0 + w * P == C:
+            k = block_of[i]
+            if k not in y_staged:
+                y_staged[k] = work.tile([P, span(k)[2] * GROUP], BF16, name="y_staged", bufs=2, align_bytes=64)
+            j0 = (c0 - span(k)[1]) // P
+            copy_bank(banks[i][:], y_staged[k][:, j0 * GROUP : (j0 + w) * GROUP], on_vector)
+
+        def quantise_y(k):
+            g, c0, w = span(k)
+            lo, hi = c0, c0 + w * P
+            nc.vector.quantize_mx(out=y_words[g][:, lo:hi].bitcast(E4M3X4), scales=y_scales[g][:, lo:hi], in_=y_staged[k][:])
+            dst = out_1[g].rearrange("p n t -> p (n t)")[:, 4 * lo : 4 * hi].bitcast(I32)
+            nc.sync.dma_start(out=dst, in_=y_words[g][:, lo:hi].bitcast(I32))
+            if hi == C:
                 for q in range(4):
                     queue = nc.scalar if (g == GROUPS - 1 and q % 2 == 0) else nc.sync
                     queue.dma_start(
                         out=out_2[g, 4 * q : 4 * q + 4, :].bitcast(I32), in_=y_scales[g][32 * q : 32 * q + 4, :].bitcast(I32)
                     )
 
-        def prep_keys(g):
-            return [(m, g, b, h) for m in range(2) for b in range(2) for h in range(PASSES)]
-
         order_words(head[0])
-        for n in range(len(head) + 1):
+        for n in range(len(head) + 2):
             if n + 1 < len(head):
                 order_words(head[n + 1])
-            if n >= 1:
-                copy_bank(head[n - 1], 2, False)
+            if 1 <= n <= len(head):
+                copy_atoms(head[n - 1], False)
             if n >= 2:
-                quantise_atoms(head[n - 2])
+                m, g, b, h = head[n - 2]
+                quantise_atoms(m, g, h, b, b + 1)
             if n < len(head):
                 turn_atoms(head[n])
-        quantise_atoms(head[-1])
 
-        pending = prep_keys(1) + prep_keys(2)
-        turned_in = {}
-        to_order = pending[:6]
-        for i, n in enumerate([2,2,2,2,0,2,2,2,2]):
-            turned_in[i] = pending[:n]
-            pending = pending[n:]
-
-        last = len(steps) - 1
-        for i in range(len(steps) + 4):
-            copies = [(key, 2) for key in turned_in.get(i - 1, [])]
-            if 0 <= i - 4:
-                copies = copies + [(i - 4, steps[i - 4][2])]
-            products = [(m, j) for m in range(2) for j in range(steps[i][2])] if i <= last else []
+        pending = [(m, g, h) for g in range(1, GROUPS) for m in range(2) for h in range(PASSES)]
+        prepared_in = dict(zip([0,1,2,3,5,6,7,8], pending))
+        to_order = pending[:2]
+        to_round = []
+        to_turn = []
+        to_copy = []
+        to_quantise = []
+        i = 0
+        while i < len(steps) or to_round or to_turn or to_copy or to_quantise or i - 1 in block_of:
+            copies = [key for key in to_copy if key not in [99]]
+            vector_copies = [key for key in to_copy if key not in copies]
+            to_copy = []
+            products = [(m, j) for m in range(2) for j in range(steps[i][2])] if i < len(steps) else []
             for n in range(max(len(copies), len(products))):
                 if n < len(copies):
-                    copy_bank(copies[n][0], copies[n][1], False)
+                    if copies[n] in block_of:
+                        copy_y(copies[n], False)
+                    else:
+                        copy_atoms(copies[n], False)
                 if n < len(products):
                     product_and_exp(i, products[n][0], products[n][1])
-            for key in turned_in.get(i, []):
-                if key in to_order:
-                    order_words(key)
-            if 0 <= i - 1 <= last:
-                subtract(i - 1)
-            if 0 <= i - 2 <= last:
-                round_y(i - 2)
-            if 0 <= i - 1 <= last:
-                weigh(i - 1)
-            for key in turned_in.get(i - 1, []):
-                quantise_atoms(key)
-            if 0 <= i - 4:
-                quantise_y(i - 4)
-            for key in turned_in.get(i, []):
-                turn_atoms(key)
-            if 0 <= i - 3 <= last:
-                turn_y(i - 3)
+            fill = []
+            if i - 1 in prepared_in:
+                fill.append(prepared_in[i - 1])
+            for key in copies + vector_copies:
+                if key in block_of and key == blocks[block_of[key]][-1]:
+                    to_quantise.append(block_of[key])
+            ready = block_of[i - 1] if i - 1 in block_of and i - 1 == blocks[block_of[i - 1]][-1] else None
+            turn_now = to_turn[: (1 if i in prepared_in else 2)]
+            to_turn = to_turn[len(turn_now) :]
+            if i in prepared_in and prepared_in[i] in to_order:
+                m, g, h = prepared_in[i]
+                for b in range(2):
+                    order_words((m, g, b, h))
+            if ready is not None:
+                subtract(ready)
+            for k in to_round:
+                round_y(k)
+                to_turn.extend(blocks[k])
+            to_round = []
+            for key in vector_copies:
+                copy_y(key, True)
+            if ready is not None:
+                weigh(ready)
+                to_round.append(ready)
+            for m, g, h in fill:
+                quantise_atoms(m, g, h, 0, 2)
+            for k in to_quantise:
+                quantise_y(k)
+            to_quantise = []
+            if i in prepared_in:
+                m, g, h = prepared_in[i]
+                for b in range(2):
+                    turn_atoms((m, g, b, h))
+                    to_copy.append((m, g, b, h))
+            for n in turn_now:
+                turn_y(n)
+                to_copy.append(n)
+            i = i + 1

@@ -64,7 +64,7 @@ def tile_mmd_witness_terms_k2_kernel(tc, g_words, g_scales, target, selected, ma
 
         def load_pass(key):
             m, g, b, h = key
-            t = keep.tile([P, 2, 512], BF16, name="raw_%d_%d_%d_%d" % key, align_bytes=64)
+            t = work.tile([P, 2, 512], BF16, name="raw_pass", bufs=8, align_bytes=64)
             a0 = g * GROUP + b * HALF
             src = atoms[m][a0 : a0 + HALF, 512 * h : 512 * (h + 1)]
             nc.sync.dma_start(out=t[:], in_=src.rearrange("(j r) k -> r j k", j=2))
@@ -96,9 +96,6 @@ def tile_mmd_witness_terms_k2_kernel(tc, g_words, g_scales, target, selected, ma
         load_atoms(1, 1, 0)
         load_g_words(2)
         load_atoms(1, 1, 1)
-        for m in range(2):
-            for b in range(2):
-                load_atoms(m, 2, b)
 
         codes = {}
         scales = {}
@@ -139,7 +136,7 @@ def tile_mmd_witness_terms_k2_kernel(tc, g_words, g_scales, target, selected, ma
         def copy_atoms(key, on_vector):
             m, g, b, h = key
             if (m, g, h) not in staged:
-                staged[(m, g, h)] = work.tile([P, 2, 4 * HALF], BF16, name="staged", bufs=3, align_bytes=64)
+                staged[(m, g, h)] = work.tile([P, 2, 4 * HALF], BF16, name="staged", bufs=4, align_bytes=64)
             copy_bank(banks[key][:], staged[(m, g, h)][:, b, :], on_vector)
 
         def quantise_atoms(m, g, h, b0, b1):
@@ -171,7 +168,7 @@ def tile_mmd_witness_terms_k2_kernel(tc, g_words, g_scales, target, selected, ma
             g, c0, w = steps[i]
             k = block_of[i]
             if (k, m) not in exps:
-                exps[(k, m)] = work.tile([P, span(k)[2], GROUP], F32, name="exp_%d" % m, bufs=3)
+                exps[(k, m)] = work.tile([P, span(k)[2], GROUP], F32, name="exp_%d" % m, bufs=4)
             c = c0 + j * P
             chunk = [n for n, (lo, hi) in enumerate(G_CHUNKS) if lo <= c < hi][0]
             off = c - G_CHUNKS[chunk][0]
@@ -190,12 +187,12 @@ def tile_mmd_witness_terms_k2_kernel(tc, g_words, g_scales, target, selected, ma
 
         def subtract(k):
             g, c0, w = span(k)
-            diffs[k] = work.tile([P, w, GROUP], F32, name="diff", bufs=1)
+            diffs[k] = work.tile([P, w, GROUP], F32, name="diff", bufs=2)
             nc.vector.tensor_tensor(out=diffs[k][:], in0=exps[(k, 0)][:], in1=exps[(k, 1)][:], op=SUB)
 
         def weigh(k):
             g, c0, w = span(k)
-            ys[k] = work.tile([P, w, GROUP], F32, name="y", bufs=3)
+            ys[k] = work.tile([P, w, GROUP], F32, name="y", bufs=16)
             row = mass_b[:, g * GROUP : (g + 1) * GROUP]
             nc.vector.tensor_tensor(out=ys[k][:], in0=diffs[k][:], in1=row.unsqueeze(1).to_broadcast([P, w, GROUP]), op=MUL)
             nc.sync.dma_start(
@@ -204,7 +201,7 @@ def tile_mmd_witness_terms_k2_kernel(tc, g_words, g_scales, target, selected, ma
 
         def round_y(k):
             g, c0, w = span(k)
-            rounded[k] = work.tile([P, w, 2, P, 2], BF16, name="rounded", bufs=2, align_bytes=64)
+            rounded[k] = work.tile([P, w, 2, P, 2], BF16, name="rounded", bufs=3, align_bytes=64)
             src = ys[k][:].rearrange("c j (p u e) -> c j u p e", u=2, e=2)
             if k in [12,13,14]:
                 nc.scalar.copy(out=rounded[k][:], in_=src)
@@ -226,7 +223,7 @@ def tile_mmd_witness_terms_k2_kernel(tc, g_words, g_scales, target, selected, ma
             g, c0, w = steps[i]
             k = block_of[i]
             if k not in y_staged:
-                y_staged[k] = work.tile([P, span(k)[2] * GROUP], BF16, name="y_staged", bufs=2, align_bytes=64)
+                y_staged[k] = work.tile([P, span(k)[2] * GROUP], BF16, name="y_staged", bufs=3, align_bytes=64)
             j0 = (c0 - span(k)[1]) // P
             copy_bank(banks[i][:], y_staged[k][:, j0 * GROUP : (j0 + w) * GROUP], on_vector)
 
@@ -255,9 +252,14 @@ def tile_mmd_witness_terms_k2_kernel(tc, g_words, g_scales, target, selected, ma
             if n < len(head):
                 turn_atoms(head[n])
 
+        for m in range(2):
+            for h in range(PASSES):
+                for b in range(2):
+                    load_pass((m, 2, b, h))
+
         pending = [(m, g, h) for g in range(1, GROUPS) for m in range(2) for h in range(PASSES)]
         prepared_in = dict(zip([0,1,2,3,5,6,7,8], pending))
-        to_order = pending[:2]
+        to_order = pending[:3]
         to_round = []
         to_turn = []
         to_copy = []

from contextlib import ExitStack

import concourse.mybir as mybir
from concourse.masks import make_identity

D, C, A = 1024, 1280, 1536
FLOPS = 2 * 2 * D * C * A

F32 = mybir.dt.float32
BF16 = mybir.dt.bfloat16
I32 = mybir.dt.int32
U32 = mybir.dt.uint32
U8 = mybir.dt.uint8
E4M3X4 = mybir.dt.float8_e4m3fn_x4
E5M2X4 = mybir.dt.float8_e5m2_x4
EXP = mybir.ActivationFunctionType.Exp
SUB = mybir.AluOpType.subtract
MUL = mybir.AluOpType.mult

P = 128
PASSES = D // 512
GROUP = 512
GROUPS = A // GROUP
HALF = GROUP // 2
G_CHUNKS = [(0, 256), (256, 768), (768, 1280)]


def tile_mmd_witness_terms_k2_kernel(tc, g_words, g_scales, target, selected, mass, out_0, out_1, out_2):
    nc = tc.nc
    atoms = [target, selected]

    steps = []
    for g in range(GROUPS):
        widths = [2, 2, 2, 2, 2] if g < GROUPS - 1 else [2, 2, 2, 2, 1, 1]
        c0 = 0
        for w in widths:
            steps.append((g, c0, w))
            c0 = c0 + w * P

    with ExitStack() as ctx:
        keep = ctx.enter_context(tc.tile_pool(name="keep", bufs=1))
        work = ctx.enter_context(tc.tile_pool(name="work", bufs=2))
        psum = ctx.enter_context(tc.psum_pool(name="psum", bufs=1))
        ctx.enter_context(tc.manual_schedule())

        ident = keep.tile([P, P], F32, name="ident")
        make_identity(nc, ident[:])
        warm_in = keep.tile([P, 1], F32, name="warm_in")
        warm_out = keep.tile([P, 1], F32, name="warm_out")
        nc.vector.memset(warm_in[:], 0.0)
        nc.scalar.activation(out=warm_out[:], in_=warm_in[:], func=EXP)
        g_sc = keep.tile([P, PASSES, C], U8, name="g_sc", align_bytes=64)
        nc.vector.memset(g_sc[:].bitcast(I32), 0)

        raw = {}
        g_w = {}

        def load_atoms(m, g, b):
            t = keep.tile([P, 2, D], BF16, name="raw_%d_%d_%d" % (m, g, b), align_bytes=64)
            a0 = g * GROUP + b * HALF
            nc.sync.dma_start(out=t[:], in_=atoms[m][a0 : a0 + HALF, :].rearrange("(j r) k -> r j k", j=2))
            for h in range(PASSES):
                raw[(m, g, b, h)] = t[:].bitcast(F32)[:, :, 256 * h : 256 * (h + 1)]

        def load_pass(key):
            m, g, b, h = key
            t = work.tile([P, 2, 512], BF16, name="raw_pass", bufs=8, align_bytes=64)
            a0 = g * GROUP + b * HALF
            src = atoms[m][a0 : a0 + HALF, 512 * h : 512 * (h + 1)]
            nc.sync.dma_start(out=t[:], in_=src.rearrange("(j r) k -> r j k", j=2))
            raw[key] = t[:].bitcast(F32)

        def load_g_words(i):
            lo, hi = G_CHUNKS[i]
            t = keep.tile([P, PASSES, hi - lo], U32, name="g_w_%d" % i, align_bytes=64)
            src = g_words.rearrange("h p n t -> p h (n t)")[:, :, 4 * lo : 4 * hi].bitcast(I32)
            nc.sync.dma_start(out=t[:].bitcast(I32), in_=src)
            g_w[i] = t

        def load_g_scales():
            for q in range(4):
                src = g_scales[:, 4 * q : 4 * q + 4, :].rearrange("h r n -> r h n").bitcast(I32)
                nc.sync.dma_start(out=g_sc[32 * q : 32 * q + 4, :, :].bitcast(I32), in_=src)

        mass_cols = keep.tile([P, GROUPS, 4], BF16, name="mass_cols", align_bytes=64)
        nc.sync.dma_start(out=mass_cols[:], in_=mass.rearrange("(g r e) -> r g e", g=GROUPS, e=4))

        head = [(m, 0, b, h) for m in range(2) for b in range(2) for h in range(PASSES)]
        for key in head:
            load_pass(key)
        load_g_words(0)
        load_g_scales()
        load_atoms(0, 1, 0)
        load_atoms(0, 1, 1)
        load_g_words(1)
        load_atoms(1, 1, 0)
        load_g_words(2)
        load_atoms(1, 1, 1)

        codes = {}
        scales = {}
        for m in range(2):
            for g in range(GROUPS):
                for h in range(PASSES):
                    codes[(m, g, h)] = keep.tile([P, GROUP], U32, name="codes_%d_%d_%d" % (m, g, h), align_bytes=64)
                    scales[(m, g, h)] = keep.tile([P, GROUP], U8, name="scales_%d_%d_%d" % (m, g, h), align_bytes=64)
        y_words = [keep.tile([P, C], U32, name="y_words_%d" % g, align_bytes=64) for g in range(GROUPS)]
        y_scales = [keep.tile([P, C], U8, name="y_scales_%d" % g, align_bytes=64) for g in range(GROUPS)]

        banks = {}
        staged = {}
        ordered = {}

        def turn_atoms(key):
            bank = psum.tile([P, 2, 2, P], F32, name="turned", bufs=3)
            for j in range(2):
                for u in range(2):
                    src = ordered[key][:, j, u, :] if key in ordered else raw[key][:, j, u : 256 : 2]
                    nc.tensor.transpose(bank[:, j, u, :], src, ident[:])
            banks[key] = bank

        def order_words(key):
            t = work.tile([P, 2, 2, P], F32, name="ordered", bufs=3)
            nc.vector.tensor_copy(out=t[:], in_=raw[key].rearrange("r j (p u) -> r j u p", u=2))
            ordered[key] = t

        def copy_bank(bank, dst, on_vector):
            w = bank.shape[1]
            dst = dst.bitcast(F32).rearrange("p (j r u) -> p j r u", j=w, u=2)
            src = bank.rearrange("p j u r -> p j r u")
            if on_vector:
                nc.vector.tensor_copy(out=dst, in_=src)
            else:
                nc.scalar.copy(out=dst, in_=src)

        def copy_atoms(key, on_vector):
            m, g, b, h = key
            if (m, g, h) not in staged:
                staged[(m, g, h)] = work.tile([P, 2, 4 * HALF], BF16, name="staged", bufs=4, align_bytes=64)
            copy_bank(banks[key][:], staged[(m, g, h)][:, b, :], on_vector)

        def quantise_atoms(m, g, h, b0, b1):
            cols = slice(b0 * HALF, b1 * HALF)
            src = staged[(m, g, h)][:, b0:b1, :].rearrange("p b n -> p (b n)")
            nc.vector.quantize_mx(out=codes[(m, g, h)][:, cols].bitcast(E4M3X4), scales=scales[(m, g, h)][:, cols], in_=src)

        mass_b = keep.tile([P, A], BF16, name="mass_b", align_bytes=64)
        for g0, g1 in ((0, 2), (2, 3)):
            bank = psum.tile([P, g1 - g0, 2, P], F32, name="turned", bufs=3)
            for g in range(g0, g1):
                for u in range(2):
                    nc.tensor.transpose(bank[:, g - g0, u, :], mass_cols[:].bitcast(F32)[:, g, u : u + 1].to_broadcast([P, P]), ident[:])
            copy_bank(bank[:], mass_b[:, g0 * GROUP : g1 * GROUP], False)

        exps = {}
        ys = {}
        diffs = {}
        rounded = {}
        y_staged = {}
        blocks = [[n] for n in range(16)]
        block_of = {i: k for k, blk in enumerate(blocks) for i in blk}

        def span(k):
            g, c0, w = steps[blocks[k][0]]
            return g, c0, sum(steps[i][2] for i in blocks[k])

        def product_and_exp(i, m, j):
            g, c0, w = steps[i]
            k = block_of[i]
            if (k, m) not in exps:
                exps[(k, m)] = work.tile([P, span(k)[2], GROUP], F32, name="exp_%d" % m, bufs=4)
            c = c0 + j * P
            chunk = [n for n, (lo, hi) in enumerate(G_CHUNKS) if lo <= c < hi][0]
            off = c - G_CHUNKS[chunk][0]
            acc = psum.tile([P, GROUP], F32, name="acc", bufs=5)
            for h in range(PASSES):
                nc.tensor.matmul_mx(
                    out=acc[:],
                    lhsT=g_w[chunk][:, h, off : off + P].bitcast(E5M2X4),
                    lhsT_scale=g_sc[:, h, c : c + P],
                    rhs=codes[(m, g, h)][:].bitcast(E4M3X4),
                    rhs_scale=scales[(m, g, h)][:],
                    start=(h == 0),
                    stop=(h == PASSES - 1),
                )
            nc.scalar.activation(out=exps[(k, m)][:, (c - span(k)[1]) // P, :], in_=acc[:], func=EXP)

        def subtract(k):
            g, c0, w = span(k)
            diffs[k] = work.tile([P, w, GROUP], F32, name="diff", bufs=2)
            nc.vector.tensor_tensor(out=diffs[k][:], in0=exps[(k, 0)][:], in1=exps[(k, 1)][:], op=SUB)

        def weigh(k):
            g, c0, w = span(k)
            ys[k] = work.tile([P, w, GROUP], F32, name="y", bufs=16)
            row = mass_b[:, g * GROUP : (g + 1) * GROUP]
            nc.vector.tensor_tensor(out=ys[k][:], in0=diffs[k][:], in1=row.unsqueeze(1).to_broadcast([P, w, GROUP]), op=MUL)
            nc.sync.dma_start(
                out=out_0[c0 : c0 + w * P, g * GROUP : (g + 1) * GROUP].rearrange("(j c) a -> c j a", j=w), in_=ys[k][:]
            )

        def round_y(k):
            g, c0, w = span(k)
            rounded[k] = work.tile([P, w, 2, P, 2], BF16, name="rounded", bufs=3, align_bytes=64)
            src = ys[k][:].rearrange("c j (p u e) -> c j u p e", u=2, e=2)
            if k in [12,13,14]:
                nc.scalar.copy(out=rounded[k][:], in_=src)
            else:
                nc.vector.tensor_copy(out=rounded[k][:], in_=src)

        def turn_y(i):
            g, c0, w = steps[i]
            k = block_of[i]
            j0 = (c0 - span(k)[1]) // P
            words = rounded[k][:].rearrange("c j u p e -> c j u (p e)").bitcast(F32)
            bank = psum.tile([P, w, 2, P], F32, name="turned", bufs=3)
            for j in range(w):
                for u in range(2):
                    nc.tensor.transpose(bank[:, j, u, :], words[:, j0 + j, u, :], ident[:])
            banks[i] = bank

        def copy_y(i, on_vector):
            g, c0, w = steps[i]
            k = block_of[i]
            if k not in y_staged:
                y_staged[k] = work.tile([P, span(k)[2] * GROUP], BF16, name="y_staged", bufs=3, align_bytes=64)
            j0 = (c0 - span(k)[1]) // P
            copy_bank(banks[i][:], y_staged[k][:, j0 * GROUP : (j0 + w) * GROUP], on_vector)

        def quantise_y(k):
            g, c0, w = span(k)
            lo, hi = c0, c0 + w * P
            nc.vector.quantize_mx(out=y_words[g][:, lo:hi].bitcast(E4M3X4), scales=y_scales[g][:, lo:hi], in_=y_staged[k][:])
            dst = out_1[g].rearrange("p n t -> p (n t)")[:, 4 * lo : 4 * hi].bitcast(I32)
            nc.sync.dma_start(out=dst, in_=y_words[g][:, lo:hi].bitcast(I32))
            if hi == C:
                for q in range(4):
                    queue = nc.scalar if (g == GROUPS - 1 and q % 2 == 0) else nc.sync
                    queue.dma_start(
                        out=out_2[g, 4 * q : 4 * q + 4, :].bitcast(I32), in_=y_scales[g][32 * q : 32 * q + 4, :].bitcast(I32)
                    )

        order_words(head[0])
        for n in range(len(head) + 2):
            if n + 1 < len(head):
                order_words(head[n + 1])
            if 1 <= n <= len(head):
                copy_atoms(head[n - 1], False)
            if n >= 2:
                m, g, b, h = head[n - 2]
                quantise_atoms(m, g, h, b, b + 1)
            if n < len(head):
                turn_atoms(head[n])

        for m in range(2):
            for h in range(PASSES):
                for b in range(2):
                    load_pass((m, 2, b, h))

        pending = [(m, g, h) for g in range(1, GROUPS) for m in range(2) for h in range(PASSES)]
        prepared_in = dict(zip([0,1,2,3,5,6,7,8], pending))
        to_order = pending[:3]
        to_round = []
        to_turn = []
        to_copy = []
        to_quantise = []
        i = 0
        while i < len(steps) or to_round or to_turn or to_copy or to_quantise or i - 1 in block_of:
            copies = [key for key in to_copy if key not in [99]]
            vector_copies = [key for key in to_copy if key not in copies]
            to_copy = []
            products = [(m, j) for m in range(2) for j in range(steps[i][2])] if i < len(steps) else []
            for n in range(max(len(copies), len(products))):
                if n < len(copies):
                    if copies[n] in block_of:
                        copy_y(copies[n], False)
                    else:
                        copy_atoms(copies[n], False)
                if n < len(products):
                    product_and_exp(i, products[n][0], products[n][1])
            fill = []
            if i - 1 in prepared_in:
                fill.append(prepared_in[i - 1])
            for key in copies + vector_copies:
                if key in block_of and key == blocks[block_of[key]][-1]:
                    to_quantise.append(block_of[key])
            ready = block_of[i - 1] if i - 1 in block_of and i - 1 == blocks[block_of[i - 1]][-1] else None
            turn_now = to_turn[: (1 if i in prepared_in else 2)]
            to_turn = to_turn[len(turn_now) :]
            if i in prepared_in and prepared_in[i] in to_order:
                m, g, h = prepared_in[i]
                for b in range(2):
                    order_words((m, g, b, h))
            if ready is not None:
                subtract(ready)
            for k in to_round:
                round_y(k)
                to_turn.extend(blocks[k])
            to_round = []
            for key in vector_copies:
                copy_y(key, True)
            if ready is not None:
                weigh(ready)
                to_round.append(ready)
            for m, g, h in fill:
                quantise_atoms(m, g, h, 0, 2)
            for k in to_quantise:
                quantise_y(k)
            to_quantise = []
            if i in prepared_in:
                m, g, h = prepared_in[i]
                for b in range(2):
                    turn_atoms((m, g, b, h))
                    to_copy.append((m, g, b, h))
            for n in turn_now:
                turn_y(n)
                to_copy.append(n)
            i = i + 1
